import numpy as np
import ml_dtypes


def mxq(x, axis, fmt="e4m3"):
    dtype, down = {"e4m3": (ml_dtypes.float8_e4m3fn, 7), "e5m2": (ml_dtypes.float8_e5m2, 14)}[fmt]
    v = np.moveaxis(np.asarray(x, np.float32).astype(ml_dtypes.bfloat16).astype(np.float64), axis, -1)
    blocks = v.reshape(v.shape[:-1] + (-1, 32))
    amax = np.abs(blocks).max(-1, keepdims=True)
    byte = np.maximum(np.where(amax > 0, np.frexp(amax)[1] - 1 + 127, 0) - down, 1)
    scale = np.exp2(byte - 127.0)
    codes = (blocks / scale).astype(np.float32).astype(dtype).astype(np.float64)
    return np.moveaxis((codes * scale).reshape(v.shape), -1, axis)


WIDE = False


def mx_kscale(k):
    if not WIDE:
        return np.ones(k)
    levels = np.array([10, -10, 5, -5, 0])
    if k % 512:
        return np.exp2(np.random.permutation(np.resize(levels, k // 32))).repeat(32)
    a = np.empty((k // 512, 16))
    for p in range(k // 512):
        a[p, :8] = np.random.permutation(np.resize(levels, 8))
        for g in range(8):
            far = levels[np.abs(levels - a[p, g]) >= 10]
            a[p, g + 8] = far[np.random.randint(len(far))]
    return np.exp2(a.ravel()).repeat(32)


def f64(x):
    return np.asarray(x).astype(np.float64)


def striped(idx):
    return np.tile(idx.reshape(-1, 16).T, (8, 1)).astype(np.uint16)


def unstriped(offs):
    return offs[:16].T.reshape(-1).astype(np.int64)


def striped8(idx):
    return np.concatenate([x.reshape(-1, 16).T for x in idx]).astype(np.uint16)


def runs(offs, k):
    lists = np.stack([offs[16 * r : 16 * r + 16].T.reshape(-1) for r in range(8)]).astype(np.int64)
    return lists[np.arange(k) % 512 // 64]


def pack_weight(w):
    k, n = w.shape
    w = f64(np.asarray(w, np.float32).astype(ml_dtypes.bfloat16)).reshape(k // 32, 32, n)
    amax = np.abs(w).max(1)
    byte = np.clip(np.where(amax > 0, np.frexp(amax)[1] - 1 + 127 - 7, 1), 1, 254)
    scaled = (w * np.exp2(127.0 - byte)[:, None, :]).reshape(k, n).astype(np.float32)
    words = np.ascontiguousarray(scaled.reshape(k // 512, 128, 4, n).transpose(0, 1, 3, 2)).astype(ml_dtypes.float8_e4m3fn).view(np.uint8)
    return words, np.ascontiguousarray(byte.astype(np.uint8).reshape(k // 512, 16, n))


def unpack_weight(words, scales):
    g, p, n, _ = words.shape
    vals = np.ascontiguousarray(words).view(ml_dtypes.float8_e4m3fn).astype(np.float64) * np.repeat(np.exp2(scales.astype(np.float64) - 127.0), 8, axis=1)[..., None]
    return vals.transpose(0, 1, 3, 2).reshape(g * 512, n)


K, T, S, N, G, H = 512, 2048, 256, 512, 2048, 512


def setup_inputs():
    n = np.random.standard_normal
    s = mx_kscale(K)[:, None]
    u = mx_kscale(K)
    packed_xT = pack_weight(n((K, T)) * s)
    packed_dT = pack_weight(n((K, G)) / s)
    return {
        "x_words": packed_xT[0],
        "x_scales": packed_xT[1],
        "d_words": packed_dT[0],
        "d_scales": packed_dT[1],
        "gn": (np.random.uniform(0.5, 1.5, (H, 1)) * u[:, None]).astype(np.float32),
        "w1": (n((H, N)) / np.sqrt(H) / u[:, None]).astype(np.float32),
        "offs": striped(np.random.permutation(T)[:S]),
        "k1": striped8(np.random.randint(0, G, (8, H))),
        "two": striped(np.random.permutation(T)[:S]),
        "n1": striped(np.random.permutation(S)),
        "n2": striped(np.random.permutation(S)),
        "n3": striped8(np.stack([np.random.permutation(S) for _ in range(8)])),
        "n4": striped8(np.stack([np.random.permutation(S) for _ in range(8)])),
    }


def reference(x_words, x_scales, d_words, d_scales, gn, w1, offs, k1, two, n1, n2, n3, n4):
    d_k1 = unpack_weight(d_words, d_scales)[np.arange(K)[:, None], runs(k1, K)]
    xq = unpack_weight(x_words, x_scales)[:, unstriped(offs)]
    a = 0.0625 * (d_k1.T @ xq)
    x_two = unpack_weight(x_words, x_scales)[:, unstriped(two)]
    b = 0.0625 * (d_k1.T @ x_two)
    z = f64(gn) * (np.maximum(a, b[:, unstriped(n2)]) - (np.minimum(a[:, unstriped(n1)], b)))
    h = mxq(f64(w1), 0, "e4m3").T @ mxq(z, 0, "e4m3")
    return np.maximum(h[np.arange(N)[:, None], runs(n3, N)], h[np.arange(N)[:, None], runs(n4, N)]) - (0.75 * h)

@@ -1,0 +1,188 @@
+from contextlib import ExitStack
+
+import concourse.mybir as mybir
+
+K, T, S, N, G, H = 512, 2048, 256, 512, 2048, 512
+FLOPS = 2 * K * H * S * 2 + 2 * H * N * S
+
+F32 = mybir.dt.float32
+BF16 = mybir.dt.bfloat16
+I32 = mybir.dt.int32
+U32 = mybir.dt.uint32
+U16 = mybir.dt.uint16
+U8 = mybir.dt.uint8
+FP8X4 = mybir.dt.float8_e4m3fn_x4
+ALU = mybir.AluOpType
+COPY = mybir.ActivationFunctionType.Copy
+
+P = 128
+PACK = 4
+
+
+def tile_picked_twksmaxbover_none_p_kernel(tc, x_words, x_scales, d_words, d_scales, gn, w1, offs, k1, two, n1, n2, n3, n4, out):
+    nc = tc.nc
+    with ExitStack() as ctx:
+        keep = ctx.enter_context(tc.tile_pool(name="keep", bufs=1))
+        psum = ctx.enter_context(tc.psum_pool(name="psum", bufs=1))
+
+        def load_list(name, src):
+            lst = keep.tile(list(src.shape), U16, name=name)
+            nc.sync.dma_start(lst[:], src)
+            return lst
+
+        def load_words(name, src):
+            words = keep.tile([P, T], I32, name=name)
+            nc.sync.dma_start(words[:], src[0].rearrange("p n t -> p (n t)").bitcast(I32))
+            return words
+
+        d_bytes = keep.tile([P, G], U8, name="d_bytes")
+        x_bytes = keep.tile([P, T], U8, name="x_bytes")
+        nc.vector.memset(d_bytes[:].bitcast(I32), 0)
+        nc.gpsimd.memset(x_bytes[:].bitcast(I32), 0)
+        nc.scalar.dma_start(d_bytes[0:P:8, :].bitcast(I32), d_scales[0].bitcast(I32))
+        nc.scalar.dma_start(x_bytes[0:P:8, :].bitcast(I32), x_scales[0].bitcast(I32))
+
+        k1_t = load_list("k1_t", k1)
+        two_t = load_list("two_t", two)
+        offs_t = load_list("offs_t", offs)
+        d_table = load_words("d_table", d_words)
+        n2_t = load_list("n2_t", n2)
+        x_table = load_words("x_table", x_words)
+        n1_t = load_list("n1_t", n1)
+        n3_t = load_list("n3_t", n3)
+        n4_t = load_list("n4_t", n4)
+
+        gain = keep.tile([P, PACK], F32, name="gain")
+        nc.gpsimd.dma_start(gain[:], gn.rearrange("(p t) o -> p (t o)", t=PACK))
+
+        planes = keep.tile([P, H + 2 * S], U8, name="planes", align_bytes=64)
+        nc.gpsimd.memset(planes[:].bitcast(I32), 0)
+        scores = keep.tile([P, (2 * PACK + 1) * S], F32, name="scores")
+        nc.gpsimd.memset(scores[:, 2 * PACK * S :], 0.0)
+
+        picked_bytes = keep.tile([P, H + 2 * S], U8, name="picked_bytes", tag="early_late")
+        dealt_bytes = keep.tile([P, H + 2 * S], U8, name="dealt_bytes")
+        nc.vector.tensor_copy(picked_bytes[:, 0:H], d_bytes[:].indirect(k1_t[:]))
+        nc.vector.tensor_copy(picked_bytes[:, H : H + S], x_bytes[:].indirect(two_t[:]))
+        nc.vector.tensor_copy(
+            dealt_bytes[:, 0:H].rearrange("p (t c i) -> p c t i", t=PACK, i=16),
+            picked_bytes[:, 0:H].rearrange("p (c i t) -> p c t i", t=PACK, i=16),
+        )
+        nc.vector.tensor_copy(picked_bytes[:, H + S :], x_bytes[:].indirect(offs_t[:]))
+        nc.vector.tensor_copy(dealt_bytes[:, H:].bitcast(I32), picked_bytes[:, H:].bitcast(I32))
+        for q in range(4):
+            nc.scalar.dma_start(
+                planes[32 * q : 32 * q + 4, :].bitcast(I32), dealt_bytes[32 * q : 32 * q + 32 : 8, :].bitcast(I32)
+            )
+
+        w_raw = keep.tile([P, PACK, N], F32, name="w_raw", tag="early_late")
+        nc.sync.dma_start(w_raw[:], w1.rearrange("(p j) c -> p j c", j=PACK))
+
+        keys_picked = keep.tile([P, H], U32, name="keys_picked")
+        keys = keep.tile([P, H], U32, name="keys", align_bytes=64)
+        tokens = keep.tile([P, 2 * S], U32, name="tokens", align_bytes=64)
+        nc.vector.tensor_copy(keys_picked[:], d_table[:].bitcast(U32).indirect(k1_t[:]))
+        nc.vector.tensor_copy(
+            keys[:].bitcast(I32).rearrange("p (t c i) -> p c t i", t=PACK, i=4),
+            keys_picked[:].bitcast(I32).rearrange("p (c i t) -> p c t i", t=PACK, i=4),
+        )
+        nc.vector.tensor_copy(tokens[:, 0:S], x_table[:].bitcast(U32).indirect(two_t[:]))
+        nc.vector.tensor_copy(tokens[:, S:], x_table[:].bitcast(U32).indirect(offs_t[:]))
+
+        def score(t, side):
+            acc = psum.tile([P, S], F32, name=f"acc{side}{t}", tag=f"bank{side}{t}")
+            nc.tensor.matmul_mx(
+                out=acc[:],
+                lhsT=keys[:, t * P : (t + 1) * P].bitcast(FP8X4),
+                lhsT_scale=planes[:, t * P : (t + 1) * P],
+                rhs=tokens[:, side * S : (side + 1) * S].bitcast(FP8X4),
+                rhs_scale=planes[:, H + side * S : H + (side + 1) * S],
+                start=True,
+                stop=True,
+            )
+            return acc
+
+        b_acc, a_acc = [], []
+        for t in range(PACK + 1):
+            if t < PACK:
+                b_acc.append(score(t, 0))
+            if t > 0:
+                a_acc.append(score(t - 1, 1))
+
+        def start_of(t, side):
+            return (2 * PACK - 1 - (2 * t + side)) * S
+
+        z_rows = keep.tile([P, PACK, S], BF16, name="z_rows")
+        h_win = [keep.tile([P, 2 * S], F32, name=f"h_win{t}") for t in range(PACK)]
+        for t in range(PACK):
+            b0, a0 = start_of(t, 0), start_of(t, 1)
+            b_far = keep.tile([P, S], F32, name=f"b_far{t}")
+            a_far = keep.tile([P, S], F32, name=f"a_far{t}")
+            low = keep.tile([P, S], F32, name=f"low{t}")
+            gap = keep.tile([P, S], F32, name=f"gap{t}")
+            high = h_win[t][:, S:]
+            nc.scalar.copy(scores[:, b0 : b0 + S], b_acc[t][:])
+            nc.scalar.activation(b_far[:], scores[:, b0 : b0 + 2 * S].indirect(n2_t[:]), COPY)
+            if t == 0:
+                nc.vector.tensor_copy(scores[:, a0 : a0 + S], a_acc[t][:])
+            else:
+                nc.scalar.copy(scores[:, a0 : a0 + S], a_acc[t][:])
+            if t < 2:
+                nc.vector.tensor_copy(a_far[:], scores[:, a0 : a0 + 2 * S].indirect(n1_t[:]))
+            else:
+                nc.scalar.activation(a_far[:], scores[:, a0 : a0 + 2 * S].indirect(n1_t[:]), COPY)
+            nc.vector.tensor_tensor(high, scores[:, a0 : a0 + S], b_far[:], ALU.max)
+            nc.vector.tensor_tensor(low[:], a_far[:], scores[:, b0 : b0 + S], ALU.min)
+            nc.vector.tensor_tensor(gap[:], high, low[:], ALU.subtract)
+            nc.vector.tensor_scalar(z_rows[:, t, :], gap[:], gain[:, t : t + 1], 0.0625, ALU.mult, ALU.mult)
+
+        w_grouped = keep.tile([P, PACK, P * PACK], BF16, name="w_grouped", align_bytes=64)
+        w_codes = keep.tile([P, N], U32, name="w_codes", align_bytes=64)
+        w_plane = keep.tile([P, N], U8, name="w_plane", align_bytes=64)
+        w_view = w_raw[:].rearrange("p j (r t c i) -> p t r c j i", r=8, t=PACK, i=4)
+        for t in range(PACK):
+            nc.scalar.copy(w_grouped[:, t, :].rearrange("p (r c i j) -> p r c j i", r=8, i=4, j=PACK), w_view[:, t])
+
+        z_grouped = keep.tile([P, S * PACK], BF16, name="z_grouped", align_bytes=64)
+        z_codes = keep.tile([P, S], U32, name="z_codes", align_bytes=64)
+        z_plane = keep.tile([P, S], U8, name="z_plane", align_bytes=64)
+        half = S // 2
+        for u in range(2):
+            nc.vector.tensor_copy(
+                z_grouped[:, u * half * PACK : (u + 1) * half * PACK].rearrange("p (c i t) -> p c t i", i=4, t=PACK),
+                z_rows[:, :, u * half : (u + 1) * half].rearrange("p t (c i) -> p c t i", i=4),
+            )
+        nc.vector.quantize_mx(out=w_codes[:, 0:P].bitcast(FP8X4), scales=w_plane[:, 0:P], in_=w_grouped[:, 0, :])
+        for u in range(2):
+            nc.vector.quantize_mx(
+                out=z_codes[:, u * half : (u + 1) * half].bitcast(FP8X4),
+                scales=z_plane[:, u * half : (u + 1) * half],
+                in_=z_grouped[:, u * half * PACK : (u + 1) * half * PACK],
+            )
+
+        out_view = out.rearrange("(r t i) j -> t r i j", r=8, t=PACK)
+        for t in range(PACK):
+            cols = slice(t * P, (t + 1) * P)
+            if t > 0:
+                nc.vector.quantize_mx(out=w_codes[:, cols].bitcast(FP8X4), scales=w_plane[:, cols], in_=w_grouped[:, t, :])
+            acc = psum.tile([P, S], F32, name=f"h_acc{t}", tag=f"bank0{t}")
+            nc.tensor.matmul_mx(
+                out=acc[:],
+                lhsT=w_codes[:, cols].bitcast(FP8X4),
+                lhsT_scale=w_plane[:, cols],
+                rhs=z_codes[:].bitcast(FP8X4),
+                rhs_scale=z_plane[:],
+                start=True,
+                stop=True,
+            )
+            nc.vector.tensor_copy(h_win[t][:, 0:S], acc[:])
+        for t in range(PACK):
+            h3 = keep.tile([P, S], F32, name=f"h3_{t}")
+            h4 = keep.tile([P, S], F32, name=f"h4_{t}")
+            top = keep.tile([P, S], F32, name=f"top{t}")
+            res = keep.tile([P, S], F32, name=f"res{t}")
+            nc.scalar.activation(h3[:], h_win[t][:].indirect(n3_t[:]), COPY)
+            nc.scalar.activation(h4[:], h_win[t][:].indirect(n4_t[:]), COPY)
+            nc.vector.tensor_tensor(top[:], h3[:], h4[:], ALU.max)
+            nc.vector.scalar_tensor_tensor(res[:], h_win[t][:, 0:S], -0.75, top[:], ALU.mult, ALU.add)
+            nc.sync.dma_start(out_view[t], res[:])

@@ -35,16 +35,18 @@ def tile_picked_twksmaxbover_none_p_kernel(tc, x_words, x_scales, d_words, d_sca
             nc.sync.dma_start(words[:], src[0].rearrange("p n t -> p (n t)").bitcast(I32))
             return words
 
-        d_bytes = keep.tile([P, G], U8, name="d_bytes")
-        x_bytes = keep.tile([P, T], U8, name="x_bytes")
-        nc.vector.memset(d_bytes[:].bitcast(I32), 0)
-        nc.gpsimd.memset(x_bytes[:].bitcast(I32), 0)
-        nc.scalar.dma_start(d_bytes[0:P:8, :].bitcast(I32), d_scales[0].bitcast(I32))
-        nc.scalar.dma_start(x_bytes[0:P:8, :].bitcast(I32), x_scales[0].bitcast(I32))
+        def load_bytes(name, src):
+            rows = keep.tile([P, T], U8, name=name)
+            nc.sync.dma_start(rows[:].bitcast(I32), src[0].bitcast(I32).unsqueeze(1).broadcast_to([16, 8, T // 4]))
+            return rows
 
+        x_bytes = keep.tile([P, T], U8, name="x_bytes")
+        nc.vector.memset(x_bytes[:].bitcast(I32), 0)
         k1_t = load_list("k1_t", k1)
+        d_bytes = load_bytes("d_bytes", d_scales)
         two_t = load_list("two_t", two)
         offs_t = load_list("offs_t", offs)
+        nc.sync.dma_start(x_bytes[0:P:8, :].bitcast(I32), x_scales[0].bitcast(I32))
         d_table = load_words("d_table", d_words)
         n2_t = load_list("n2_t", n2)
         x_table = load_words("x_table", x_words)
@@ -52,39 +54,45 @@ def tile_picked_twksmaxbover_none_p_kernel(tc, x_words, x_scales, d_words, d_sca
         n3_t = load_list("n3_t", n3)
         n4_t = load_list("n4_t", n4)
 
-        gain = keep.tile([P, PACK], F32, name="gain")
-        nc.gpsimd.dma_start(gain[:], gn.rearrange("(p t) o -> p (t o)", t=PACK))
-
         planes = keep.tile([P, H + 2 * S], U8, name="planes", align_bytes=64)
-        nc.gpsimd.memset(planes[:].bitcast(I32), 0)
+        nc.vector.memset(planes[:].bitcast(I32), 0)
         scores = keep.tile([P, (2 * PACK + 1) * S], F32, name="scores")
-        nc.gpsimd.memset(scores[:, 2 * PACK * S :], 0.0)
+        nc.vector.memset(scores[:, 2 * PACK * S :], 0.0)
 
-        picked_bytes = keep.tile([P, H + 2 * S], U8, name="picked_bytes", tag="early_late")
-        dealt_bytes = keep.tile([P, H + 2 * S], U8, name="dealt_bytes")
-        nc.vector.tensor_copy(picked_bytes[:, 0:H], d_bytes[:].indirect(k1_t[:]))
-        nc.vector.tensor_copy(picked_bytes[:, H : H + S], x_bytes[:].indirect(two_t[:]))
+        key_bytes = keep.tile([P, H], U8, name="key_bytes")
+        token_bytes = keep.tile([P, 2 * S], U8, name="token_bytes", tag="bytes_then_keys")
+        dealt_bytes = keep.tile([P, H + 2 * S], U8, name="dealt_bytes", tag="dealt_then_w")
+        nc.vector.tensor_copy(key_bytes[:], d_bytes[:].indirect(k1_t[:]))
+        nc.vector.tensor_copy(token_bytes[:, 0:S], x_bytes[:].indirect(two_t[:]))
+        nc.vector.tensor_copy(token_bytes[:, S:], x_bytes[:].indirect(offs_t[:]))
         nc.vector.tensor_copy(
-            dealt_bytes[:, 0:H].rearrange("p (t c i) -> p c t i", t=PACK, i=16),
-            picked_bytes[:, 0:H].rearrange("p (c i t) -> p c t i", t=PACK, i=16),
+            dealt_bytes[:, 0:H].bitcast(I32).rearrange("p (t g s) -> p g t s", t=PACK, s=2),
+            key_bytes[:].bitcast(I32).rearrange("p (g t s) -> p g t s", t=PACK, s=2),
         )
-        nc.vector.tensor_copy(picked_bytes[:, H + S :], x_bytes[:].indirect(offs_t[:]))
-        nc.vector.tensor_copy(dealt_bytes[:, H:].bitcast(I32), picked_bytes[:, H:].bitcast(I32))
+        nc.vector.tensor_copy(dealt_bytes[:, H:].bitcast(I32), token_bytes[:].bitcast(I32))
         for q in range(4):
             nc.scalar.dma_start(
                 planes[32 * q : 32 * q + 4, :].bitcast(I32), dealt_bytes[32 * q : 32 * q + 32 : 8, :].bitcast(I32)
             )
 
-        w_raw = keep.tile([P, PACK, N], F32, name="w_raw", tag="early_late")
-        nc.sync.dma_start(w_raw[:], w1.rearrange("(p j) c -> p j c", j=PACK))
+        late = keep.tile([P, PACK * (N + 8)], F32, name="late", tag="dealt_then_w")
+        gain = late[:, PACK * N :].rearrange("p (t e) -> p t e", e=8)
+        w_raw = late[:, 0 : PACK * N].rearrange("p (j c) -> p j c", j=PACK)
+        gn_view = gn.rearrange("(g t s) o -> t g s o", t=PACK, s=8)
+        with nc.allow_non_contiguous_dma(reason="one gain a partition"):
+            for t in range(PACK):
+                nc.sync.dma_start(gain[:, t, 0:1], gn_view[t])
+        w1_view = w1.rearrange("(g j s) c -> j g s c", j=PACK, s=8)
+        for j in range(PACK):
+            nc.sync.dma_start(w_raw[:, j, :], w1_view[j])
 
-        keys_picked = keep.tile([P, H], U32, name="keys_picked")
+        keys_picked = keep.tile([P, H], U32, name="keys_picked", tag="bytes_then_keys")
         keys = keep.tile([P, H], U32, name="keys", align_bytes=64)
         tokens = keep.tile([P, 2 * S], U32, name="tokens", align_bytes=64)
         nc.vector.tensor_copy(keys_picked[:], d_table[:].bitcast(U32).indirect(k1_t[:]))
         nc.vector.tensor_copy(
-            keys[:].bitcast(I32).rearrange("p (t c i) -> p c t i", t=PACK, i=4),
-            keys_picked[:].bitcast(I32).rearrange("p (c i t) -> p c t i", t=PACK, i=4),
+            keys[:].bitcast(I32).rearrange("p (t g s) -> p g t s", t=PACK, s=8),
+            keys_picked[:].bitcast(I32).rearrange("p (g t s) -> p g t s", t=PACK, s=8),
         )
         nc.vector.tensor_copy(tokens[:, 0:S], x_table[:].bitcast(U32).indirect(two_t[:]))
         nc.vector.tensor_copy(tokens[:, S:], x_table[:].bitcast(U32).indirect(offs_t[:]))
@@ -116,10 +124,10 @@ def tile_picked_twksmaxbover_none_p_kernel(tc, x_words, x_scales, d_words, d_sca
         h_win = [keep.tile([P, 2 * S], F32, name=f"h_win{t}") for t in range(PACK)]
         for t in range(PACK):
             b0, a0 = start_of(t, 0), start_of(t, 1)
-            b_far = keep.tile([P, S], F32, name=f"b_far{t}")
-            a_far = keep.tile([P, S], F32, name=f"a_far{t}")
-            low = keep.tile([P, S], F32, name=f"low{t}")
-            gap = keep.tile([P, S], F32, name=f"gap{t}")
+            b_far = keep.tile([P, S], F32, name=f"b_far{t}", align_bytes=64)
+            a_far = keep.tile([P, S], F32, name=f"a_far{t}", align_bytes=64)
+            low = keep.tile([P, S], F32, name=f"low{t}", align_bytes=64)
+            gap = keep.tile([P, S], F32, name=f"gap{t}", align_bytes=64)
             high = h_win[t][:, S:]
             nc.scalar.copy(scores[:, b0 : b0 + S], b_acc[t][:])
             nc.scalar.activation(b_far[:], scores[:, b0 : b0 + 2 * S].indirect(n2_t[:]), COPY)
@@ -134,14 +142,15 @@ def tile_picked_twksmaxbover_none_p_kernel(tc, x_words, x_scales, d_words, d_sca
             nc.vector.tensor_tensor(high, scores[:, a0 : a0 + S], b_far[:], ALU.max)
             nc.vector.tensor_tensor(low[:], a_far[:], scores[:, b0 : b0 + S], ALU.min)
             nc.vector.tensor_tensor(gap[:], high, low[:], ALU.subtract)
-            nc.vector.tensor_scalar(z_rows[:, t, :], gap[:], gain[:, t : t + 1], 0.0625, ALU.mult, ALU.mult)
+            nc.vector.tensor_scalar(z_rows[:, t, :], gap[:], gain[:, t, 0:1], 0.0625, ALU.mult, ALU.mult)
 
-        w_grouped = keep.tile([P, PACK, P * PACK], BF16, name="w_grouped", align_bytes=64)
+        freed = ["b_far3", "a_far3", "low3", "gap3"]
+        w_grouped = [keep.tile([P, P * PACK], BF16, name=f"w_grouped{t}", tag=freed[t], align_bytes=64) for t in range(PACK)]
         w_codes = keep.tile([P, N], U32, name="w_codes", align_bytes=64)
         w_plane = keep.tile([P, N], U8, name="w_plane", align_bytes=64)
-        w_view = w_raw[:].rearrange("p j (r t c i) -> p t r c j i", r=8, t=PACK, i=4)
-        for t in range(PACK):
-            nc.scalar.copy(w_grouped[:, t, :].rearrange("p (r c i j) -> p r c j i", r=8, i=4, j=PACK), w_view[:, t])
+        w_view = w_raw.rearrange("p j (r t c i) -> p t r c j i", r=8, t=PACK, i=4)
+        for t in range(PACK - 1):
+            nc.scalar.copy(w_grouped[t][:].rearrange("p (r c i j) -> p r c j i", r=8, i=4, j=PACK), w_view[:, t])
 
         z_grouped = keep.tile([P, S * PACK], BF16, name="z_grouped", align_bytes=64)
         z_codes = keep.tile([P, S], U32, name="z_codes", align_bytes=64)
@@ -152,7 +161,7 @@ def tile_picked_twksmaxbover_none_p_kernel(tc, x_words, x_scales, d_words, d_sca
                 z_grouped[:, u * half * PACK : (u + 1) * half * PACK].rearrange("p (c i t) -> p c t i", i=4, t=PACK),
                 z_rows[:, :, u * half : (u + 1) * half].rearrange("p t (c i) -> p c t i", i=4),
             )
-        nc.vector.quantize_mx(out=w_codes[:, 0:P].bitcast(FP8X4), scales=w_plane[:, 0:P], in_=w_grouped[:, 0, :])
+        nc.vector.quantize_mx(out=w_codes[:, 0:P].bitcast(FP8X4), scales=w_plane[:, 0:P], in_=w_grouped[0][:])
         for u in range(2):
             nc.vector.quantize_mx(
                 out=z_codes[:, u * half : (u + 1) * half].bitcast(FP8X4),
@@ -163,8 +172,10 @@ def tile_picked_twksmaxbover_none_p_kernel(tc, x_words, x_scales, d_words, d_sca
         out_view = out.rearrange("(r t i) j -> t r i j", r=8, t=PACK)
         for t in range(PACK):
             cols = slice(t * P, (t + 1) * P)
+            if t == PACK - 1:
+                nc.vector.tensor_copy(w_grouped[t][:].rearrange("p (r c i j) -> p r c j i", r=8, i=4, j=PACK), w_view[:, t])
             if t > 0:
-                nc.vector.quantize_mx(out=w_codes[:, cols].bitcast(FP8X4), scales=w_plane[:, cols], in_=w_grouped[:, t, :])
+                nc.vector.quantize_mx(out=w_codes[:, cols].bitcast(FP8X4), scales=w_plane[:, cols], in_=w_grouped[t][:])
             acc = psum.tile([P, S], F32, name=f"h_acc{t}", tag=f"bank0{t}")
             nc.tensor.matmul_mx(
                 out=acc[:],
@@ -176,13 +187,14 @@ def tile_picked_twksmaxbover_none_p_kernel(tc, x_words, x_scales, d_words, d_sca
                 stop=True,
             )
             nc.vector.tensor_copy(h_win[t][:, 0:S], acc[:])
-        for t in range(PACK):
-            h3 = keep.tile([P, S], F32, name=f"h3_{t}")
-            h4 = keep.tile([P, S], F32, name=f"h4_{t}")
-            top = keep.tile([P, S], F32, name=f"top{t}")
-            res = keep.tile([P, S], F32, name=f"res{t}")
-            nc.scalar.activation(h3[:], h_win[t][:].indirect(n3_t[:]), COPY)
-            nc.scalar.activation(h4[:], h_win[t][:].indirect(n4_t[:]), COPY)
+        pieces = [(t, 0, S) for t in range(PACK - 1)] + [(PACK - 1, 0, half), (PACK - 1, half, S)]
+        for t, lo, hi in pieces:
+            h3 = keep.tile([P, hi - lo], F32, name=f"h3_{t}_{lo}")
+            h4 = keep.tile([P, hi - lo], F32, name=f"h4_{t}_{lo}")
+            top = keep.tile([P, hi - lo], F32, name=f"top{t}_{lo}")
+            res = keep.tile([P, hi - lo], F32, name=f"res{t}_{lo}")
+            nc.scalar.activation(h3[:], h_win[t][:].indirect(n3_t[:, lo // 16 : hi // 16]), COPY)
+            nc.scalar.activation(h4[:], h_win[t][:].indirect(n4_t[:, lo // 16 : hi // 16]), COPY)
             nc.vector.tensor_tensor(top[:], h3[:], h4[:], ALU.max)
-            nc.vector.scalar_tensor_tensor(res[:], h_win[t][:, 0:S], -0.75, top[:], ALU.mult, ALU.add)
-            nc.sync.dma_start(out_view[t], res[:])
+            nc.vector.scalar_tensor_tensor(res[:], h_win[t][:, lo:hi], -0.75, top[:], ALU.mult, ALU.add)
+            nc.sync.dma_start(out_view[t][:, :, lo:hi], res[:])

@@ -61,7 +61,7 @@ def tile_picked_twksmaxbover_none_p_kernel(tc, x_words, x_scales, d_words, d_sca
 
         key_bytes = keep.tile([P, H], U8, name="key_bytes")
         token_bytes = keep.tile([P, 2 * S], U8, name="token_bytes", tag="bytes_then_keys")
-        dealt_bytes = keep.tile([P, H + 2 * S], U8, name="dealt_bytes", tag="dealt_then_w")
+        dealt_bytes = keep.tile([P, H + 2 * S], U8, name="dealt_bytes")
         nc.vector.tensor_copy(key_bytes[:], d_bytes[:].indirect(k1_t[:]))
         nc.vector.tensor_copy(token_bytes[:, 0:S], x_bytes[:].indirect(two_t[:]))
         nc.vector.tensor_copy(token_bytes[:, S:], x_bytes[:].indirect(offs_t[:]))
@@ -75,7 +75,18 @@ def tile_picked_twksmaxbover_none_p_kernel(tc, x_words, x_scales, d_words, d_sca
                 planes[32 * q : 32 * q + 4, :].bitcast(I32), dealt_bytes[32 * q : 32 * q + 32 : 8, :].bitcast(I32)
             )
 
-        late = keep.tile([P, PACK * (N + 8)], F32, name="late", tag="dealt_then_w")
+        keys_picked = keep.tile([P, H], U32, name="keys_picked", tag="bytes_then_keys")
+        keys = keep.tile([P, H], U32, name="keys", align_bytes=64)
+        tokens = keep.tile([P, 2 * S], U32, name="tokens", align_bytes=64)
+        nc.vector.tensor_copy(keys_picked[:], d_table[:].bitcast(U32).indirect(k1_t[:]))
+        nc.vector.tensor_copy(
+            keys[:].bitcast(I32).rearrange("p (t g s) -> p g t s", t=PACK, s=8),
+            keys_picked[:].bitcast(I32).rearrange("p (g t s) -> p g t s", t=PACK, s=8),
+        )
+        nc.vector.tensor_copy(tokens[:, S:], x_table[:].bitcast(U32).indirect(offs_t[:]))
+        nc.vector.tensor_copy(tokens[:, 0:S], x_table[:].bitcast(U32).indirect(two_t[:]))
+
+        late = keep.tile([P, PACK * (N + 8)], F32, name="late", tag="d_table")
         gain = late[:, PACK * N :].rearrange("p (t e) -> p t e", e=8)
         w_raw = late[:, 0 : PACK * N].rearrange("p (j c) -> p j c", j=PACK)
         gn_view = gn.rearrange("(g t s) o -> t g s o", t=PACK, s=8)
@@ -85,17 +96,6 @@ def tile_picked_twksmaxbover_none_p_kernel(tc, x_words, x_scales, d_words, d_sca
         w1_view = w1.rearrange("(g j s) c -> j g s c", j=PACK, s=8)
         for j in range(PACK):
             nc.sync.dma_start(w_raw[:, j, :], w1_view[j])
-
-        keys_picked = keep.tile([P, H], U32, name="keys_picked", tag="bytes_then_keys")
-        keys = keep.tile([P, H], U32, name="keys", align_bytes=64)
-        tokens = keep.tile([P, 2 * S], U32, name="tokens", align_bytes=64)
-        nc.vector.tensor_copy(keys_picked[:], d_table[:].bitcast(U32).indirect(k1_t[:]))
-        nc.vector.tensor_copy(
-            keys[:].bitcast(I32).rearrange("p (t g s) -> p g t s", t=PACK, s=8),
-            keys_picked[:].bitcast(I32).rearrange("p (g t s) -> p g t s", t=PACK, s=8),
-        )
-        nc.vector.tensor_copy(tokens[:, 0:S], x_table[:].bitcast(U32).indirect(two_t[:]))
-        nc.vector.tensor_copy(tokens[:, S:], x_table[:].bitcast(U32).indirect(offs_t[:]))
 
         def score(t, side):
             acc = psum.tile([P, S], F32, name=f"acc{side}{t}", tag=f"bank{side}{t}")
@@ -113,80 +113,131 @@ def tile_picked_twksmaxbover_none_p_kernel(tc, x_words, x_scales, d_words, d_sca
         b_acc, a_acc = [], []
         for t in range(PACK + 1):
             if t < PACK:
-                b_acc.append(score(t, 0))
+                a_acc.append(score(t, 1))
             if t > 0:
-                a_acc.append(score(t - 1, 1))
+                b_acc.append(score(t - 1, 0))
 
         def start_of(t, side):
-            return (2 * PACK - 1 - (2 * t + side)) * S
+            return (2 * PACK - 1 - (2 * t + 1 - side)) * S
 
+        z_grouped = keep.tile([P, S * PACK], BF16, name="z_grouped", align_bytes=64)
         z_rows = keep.tile([P, PACK, S], BF16, name="z_rows")
+        half = S // 2
+        halves = [(0, half), (half, S)]
         h_win = [keep.tile([P, 2 * S], F32, name=f"h_win{t}") for t in range(PACK)]
-        for t in range(PACK):
-            b0, a0 = start_of(t, 0), start_of(t, 1)
-            b_far = keep.tile([P, S], F32, name=f"b_far{t}", align_bytes=64)
-            a_far = keep.tile([P, S], F32, name=f"a_far{t}", align_bytes=64)
-            low = keep.tile([P, S], F32, name=f"low{t}", align_bytes=64)
-            gap = keep.tile([P, S], F32, name=f"gap{t}", align_bytes=64)
-            high = h_win[t][:, S:]
-            nc.scalar.copy(scores[:, b0 : b0 + S], b_acc[t][:])
-            nc.scalar.activation(b_far[:], scores[:, b0 : b0 + 2 * S].indirect(n2_t[:]), COPY)
-            if t == 0:
-                nc.vector.tensor_copy(scores[:, a0 : a0 + S], a_acc[t][:])
-            else:
-                nc.scalar.copy(scores[:, a0 : a0 + S], a_acc[t][:])
-            if t < 2:
-                nc.vector.tensor_copy(a_far[:], scores[:, a0 : a0 + 2 * S].indirect(n1_t[:]))
-            else:
-                nc.scalar.activation(a_far[:], scores[:, a0 : a0 + 2 * S].indirect(n1_t[:]), COPY)
-            nc.vector.tensor_tensor(high, scores[:, a0 : a0 + S], b_far[:], ALU.max)
-            nc.vector.tensor_tensor(low[:], a_far[:], scores[:, b0 : b0 + S], ALU.min)
-            nc.vector.tensor_tensor(gap[:], high, low[:], ALU.subtract)
-            nc.vector.tensor_scalar(z_rows[:, t, :], gap[:], gain[:, t, 0:1], 0.0625, ALU.mult, ALU.mult)
+        b_far = [keep.tile([P, S], F32, name=f"b_far{t}", align_bytes=64) for t in range(PACK)]
+        a_far = [keep.tile([P, S], F32, name=f"a_far{t}", align_bytes=64) for t in range(PACK)]
+        low = [keep.tile([P, S], F32, name=f"low{t}", align_bytes=64) for t in range(PACK)]
+        gap = [keep.tile([P, S], F32, name=f"gap{t}", align_bytes=64) for t in range(PACK)]
 
-        freed = ["b_far3", "a_far3", "low3", "gap3"]
-        w_grouped = [keep.tile([P, P * PACK], BF16, name=f"w_grouped{t}", tag=freed[t], align_bytes=64) for t in range(PACK)]
+        def spans(t):
+            return halves if t == PACK - 1 else [(0, S)]
+
+        def leave_b(t):
+            b0 = start_of(t, 0)
+            nc.scalar.copy(scores[:, b0 : b0 + S], b_acc[t][:])
+
+        def leave_a(t):
+            a0 = start_of(t, 1)
+            nc.scalar.copy(scores[:, a0 : a0 + S], a_acc[t][:])
+
+        def fetch_b(t):
+            b0 = start_of(t, 0)
+            for lo, hi in spans(t):
+                picked = scores[:, b0 : b0 + 2 * S].indirect(n2_t[:, lo // 16 : hi // 16])
+                nc.scalar.activation(b_far[t][:, lo:hi], picked, COPY)
+
+        def fetch_a(t):
+            a0 = start_of(t, 1)
+            picked = scores[:, a0 : a0 + 2 * S].indirect(n1_t[:])
+            if t < 3:
+                nc.vector.tensor_copy(a_far[t][:], picked)
+            else:
+                nc.scalar.activation(a_far[t][:], picked, COPY)
+
+        def larger(t):
+            a0 = start_of(t, 1)
+            for lo, hi in spans(t):
+                nc.vector.tensor_tensor(h_win[t][:, S + lo : S + hi], scores[:, a0 + lo : a0 + hi], b_far[t][:, lo:hi], ALU.max)
+
+        def smaller(t):
+            b0 = start_of(t, 0)
+            nc.vector.tensor_tensor(low[t][:], a_far[t][:], scores[:, b0 : b0 + S], ALU.min)
+
+        def subtract(t):
+            for lo, hi in spans(t):
+                nc.vector.tensor_tensor(gap[t][:, lo:hi], h_win[t][:, S + lo : S + hi], low[t][:, lo:hi], ALU.subtract)
+
+        def scale(t):
+            for lo, hi in spans(t):
+                nc.vector.tensor_scalar(z_rows[:, t, lo:hi], gap[t][:, lo:hi], gain[:, t, 0:1], 0.0625, ALU.mult, ALU.mult)
+
+        leave_a(0)
+        for t in range(PACK + 1):
+            if t < PACK:
+                leave_b(t)
+            if t + 1 < PACK:
+                leave_a(t + 1)
+            if t < PACK:
+                fetch_a(t)
+                fetch_b(t)
+                smaller(t)
+            if t > 0:
+                subtract(t - 1)
+            if t < PACK:
+                larger(t)
+            if t > 0:
+                scale(t - 1)
+
+        freed = ["a_far3", "b_far3", "low3", "z_grouped"]
+        w_grouped = {}
         w_codes = keep.tile([P, N], U32, name="w_codes", align_bytes=64)
         w_plane = keep.tile([P, N], U8, name="w_plane", align_bytes=64)
         w_view = w_raw.rearrange("p j (r t c i) -> p t r c j i", r=8, t=PACK, i=4)
-        for t in range(PACK - 1):
-            nc.scalar.copy(w_grouped[t][:].rearrange("p (r c i j) -> p r c j i", r=8, i=4, j=PACK), w_view[:, t])
 
-        z_grouped = keep.tile([P, S * PACK], BF16, name="z_grouped", align_bytes=64)
+        def group_w(t, copy):
+            w_grouped[t] = keep.tile([P, P * PACK], BF16, name=f"w_grouped{t}", tag=freed[t], align_bytes=64)
+            copy(w_grouped[t][:].rearrange("p (r c i j) -> p r c j i", r=8, i=4, j=PACK), w_view[:, t])
+
+        def quantize_w(t):
+            cols = slice(t * P, (t + 1) * P)
+            nc.vector.quantize_mx(out=w_codes[:, cols].bitcast(FP8X4), scales=w_plane[:, cols], in_=w_grouped[t][:])
+
+        for t in range(3):
+            group_w(t, nc.scalar.copy)
+
         z_codes = keep.tile([P, S], U32, name="z_codes", align_bytes=64)
         z_plane = keep.tile([P, S], U8, name="z_plane", align_bytes=64)
-        half = S // 2
-        for u in range(2):
+        for lo, hi in halves:
             nc.vector.tensor_copy(
-                z_grouped[:, u * half * PACK : (u + 1) * half * PACK].rearrange("p (c i t) -> p c t i", i=4, t=PACK),
-                z_rows[:, :, u * half : (u + 1) * half].rearrange("p t (c i) -> p c t i", i=4),
+                z_grouped[:, lo * PACK : hi * PACK].rearrange("p (c i t) -> p c t i", i=4, t=PACK),
+                z_rows[:, :, lo:hi].rearrange("p t (c i) -> p c t i", i=4),
             )
-        nc.vector.quantize_mx(out=w_codes[:, 0:P].bitcast(FP8X4), scales=w_plane[:, 0:P], in_=w_grouped[0][:])
-        for u in range(2):
+        quantize_w(0)
+        for lo, hi in halves:
             nc.vector.quantize_mx(
-                out=z_codes[:, u * half : (u + 1) * half].bitcast(FP8X4),
-                scales=z_plane[:, u * half : (u + 1) * half],
-                in_=z_grouped[:, u * half * PACK : (u + 1) * half * PACK],
+                out=z_codes[:, lo:hi].bitcast(FP8X4), scales=z_plane[:, lo:hi], in_=z_grouped[:, lo * PACK : hi * PACK]
             )
 
         out_view = out.rearrange("(r t i) j -> t r i j", r=8, t=PACK)
         for t in range(PACK):
             cols = slice(t * P, (t + 1) * P)
-            if t == PACK - 1:
-                nc.vector.tensor_copy(w_grouped[t][:].rearrange("p (r c i j) -> p r c j i", r=8, i=4, j=PACK), w_view[:, t])
+            if t >= 3:
+                group_w(t, nc.vector.tensor_copy)
             if t > 0:
-                nc.vector.quantize_mx(out=w_codes[:, cols].bitcast(FP8X4), scales=w_plane[:, cols], in_=w_grouped[t][:])
-            acc = psum.tile([P, S], F32, name=f"h_acc{t}", tag=f"bank0{t}")
-            nc.tensor.matmul_mx(
-                out=acc[:],
-                lhsT=w_codes[:, cols].bitcast(FP8X4),
-                lhsT_scale=w_plane[:, cols],
-                rhs=z_codes[:].bitcast(FP8X4),
-                rhs_scale=z_plane[:],
-                start=True,
-                stop=True,
-            )
-            nc.vector.tensor_copy(h_win[t][:, 0:S], acc[:])
+                quantize_w(t)
+            for u, (lo, hi) in enumerate(halves if t == 0 else [(0, S)]):
+                acc = psum.tile([P, hi - lo], F32, name=f"h_acc{t}{u}", tag=f"bank{u}{t}")
+                nc.tensor.matmul_mx(
+                    out=acc[:],
+                    lhsT=w_codes[:, cols].bitcast(FP8X4),
+                    lhsT_scale=w_plane[:, cols],
+                    rhs=z_codes[:, lo:hi].bitcast(FP8X4),
+                    rhs_scale=z_plane[:, lo:hi],
+                    start=True,
+                    stop=True,
+                )
+                nc.vector.tensor_copy(h_win[t][:, lo:hi], acc[:])
         pieces = [(t, 0, S) for t in range(PACK - 1)] + [(PACK - 1, 0, half), (PACK - 1, half, S)]
         for t, lo, hi in pieces:
             h3 = keep.tile([P, hi - lo], F32, name=f"h3_{t}_{lo}")

from contextlib import ExitStack

import concourse.mybir as mybir

K, T, S, N, G, H = 512, 2048, 256, 512, 2048, 512
FLOPS = 2 * K * H * S * 2 + 2 * H * N * S

F32 = mybir.dt.float32
BF16 = mybir.dt.bfloat16
I32 = mybir.dt.int32
U32 = mybir.dt.uint32
U16 = mybir.dt.uint16
U8 = mybir.dt.uint8
FP8X4 = mybir.dt.float8_e4m3fn_x4
ALU = mybir.AluOpType
COPY = mybir.ActivationFunctionType.Copy

P = 128
PACK = 4


def tile_picked_twksmaxbover_none_p_kernel(tc, x_words, x_scales, d_words, d_scales, gn, w1, offs, k1, two, n1, n2, n3, n4, out):
    nc = tc.nc
    with ExitStack() as ctx:
        keep = ctx.enter_context(tc.tile_pool(name="keep", bufs=1))
        psum = ctx.enter_context(tc.psum_pool(name="psum", bufs=1))

        def load_list(name, src):
            lst = keep.tile(list(src.shape), U16, name=name)
            nc.sync.dma_start(lst[:], src)
            return lst

        def load_words(name, src):
            words = keep.tile([P, T], I32, name=name)
            nc.sync.dma_start(words[:], src[0].rearrange("p n t -> p (n t)").bitcast(I32))
            return words

        def load_bytes(name, src):
            rows = keep.tile([P, T], U8, name=name)
            nc.sync.dma_start(rows[:].bitcast(I32), src[0].bitcast(I32).unsqueeze(1).broadcast_to([16, 8, T // 4]))
            return rows

        x_bytes = keep.tile([P, T], U8, name="x_bytes")
        nc.vector.memset(x_bytes[:].bitcast(I32), 0)
        k1_t = load_list("k1_t", k1)
        d_bytes = load_bytes("d_bytes", d_scales)
        two_t = load_list("two_t", two)
        offs_t = load_list("offs_t", offs)
        nc.sync.dma_start(x_bytes[0:P:8, :].bitcast(I32), x_scales[0].bitcast(I32))
        d_table = load_words("d_table", d_words)
        n2_t = load_list("n2_t", n2)
        x_table = load_words("x_table", x_words)
        n1_t = load_list("n1_t", n1)
        n3_t = load_list("n3_t", n3)
        n4_t = load_list("n4_t", n4)

        planes = keep.tile([P, H + 2 * S], U8, name="planes", align_bytes=64)
        nc.vector.memset(planes[:].bitcast(I32), 0)
        scores = keep.tile([P, (2 * PACK + 1) * S], F32, name="scores")
        nc.vector.memset(scores[:, 2 * PACK * S :], 0.0)

        key_bytes = keep.tile([P, H], U8, name="key_bytes")
        token_bytes = keep.tile([P, 2 * S], U8, name="token_bytes", tag="bytes_then_keys")
        dealt_bytes = keep.tile([P, H + 2 * S], U8, name="dealt_bytes")
        nc.vector.tensor_copy(key_bytes[:], d_bytes[:].indirect(k1_t[:]))
        nc.vector.tensor_copy(token_bytes[:, 0:S], x_bytes[:].indirect(two_t[:]))
        nc.vector.tensor_copy(token_bytes[:, S:], x_bytes[:].indirect(offs_t[:]))
        nc.vector.tensor_copy(
            dealt_bytes[:, 0:H].bitcast(I32).rearrange("p (t g s) -> p g t s", t=PACK, s=2),
            key_bytes[:].bitcast(I32).rearrange("p (g t s) -> p g t s", t=PACK, s=2),
        )
        nc.vector.tensor_copy(dealt_bytes[:, H:].bitcast(I32), token_bytes[:].bitcast(I32))
        for q in range(4):
            nc.scalar.dma_start(
                planes[32 * q : 32 * q + 4, :].bitcast(I32), dealt_bytes[32 * q : 32 * q + 32 : 8, :].bitcast(I32)
            )

        keys_picked = keep.tile([P, H], U32, name="keys_picked", tag="bytes_then_keys")
        keys = keep.tile([P, H], U32, name="keys", align_bytes=64)
        tokens = keep.tile([P, 2 * S], U32, name="tokens", align_bytes=64)
        nc.vector.tensor_copy(keys_picked[:], d_table[:].bitcast(U32).indirect(k1_t[:]))
        nc.vector.tensor_copy(
            keys[:].bitcast(I32).rearrange("p (t g s) -> p g t s", t=PACK, s=8),
            keys_picked[:].bitcast(I32).rearrange("p (g t s) -> p g t s", t=PACK, s=8),
        )
        nc.vector.tensor_copy(tokens[:, S:], x_table[:].bitcast(U32).indirect(offs_t[:]))
        nc.vector.tensor_copy(tokens[:, 0:S], x_table[:].bitcast(U32).indirect(two_t[:]))

        late = keep.tile([P, PACK * (N + 8)], F32, name="late", tag="d_table")
        gain = late[:, PACK * N :].rearrange("p (t e) -> p t e", e=8)
        w_raw = late[:, 0 : PACK * N].rearrange("p (j c) -> p j c", j=PACK)
        gn_view = gn.rearrange("(g t s) o -> t g s o", t=PACK, s=8)
        with nc.allow_non_contiguous_dma(reason="one gain a partition"):
            for t in range(PACK):
                nc.sync.dma_start(gain[:, t, 0:1], gn_view[t])
        w1_view = w1.rearrange("(g j s) c -> j g s c", j=PACK, s=8)
        for j in range(PACK):
            nc.sync.dma_start(w_raw[:, j, :], w1_view[j])

        def score(t, side):
            acc = psum.tile([P, S], F32, name=f"acc{side}{t}", tag=f"bank{side}{t}")
            nc.tensor.matmul_mx(
                out=acc[:],
                lhsT=keys[:, t * P : (t + 1) * P].bitcast(FP8X4),
                lhsT_scale=planes[:, t * P : (t + 1) * P],
                rhs=tokens[:, side * S : (side + 1) * S].bitcast(FP8X4),
                rhs_scale=planes[:, H + side * S : H + (side + 1) * S],
                start=True,
                stop=True,
            )
            return acc

        b_acc, a_acc = [], []
        for t in range(PACK + 1):
            if t < PACK:
                a_acc.append(score(t, 1))
            if t > 0:
                b_acc.append(score(t - 1, 0))

        def start_of(t, side):
            return (2 * PACK - 1 - (2 * t + 1 - side)) * S

        z_grouped = keep.tile([P, S * PACK], BF16, name="z_grouped", align_bytes=64)
        z_rows = keep.tile([P, PACK, S], BF16, name="z_rows")
        half = S // 2
        halves = [(0, half), (half, S)]
        h_win = [keep.tile([P, 2 * S], F32, name=f"h_win{t}") for t in range(PACK)]
        b_far = [keep.tile([P, S], F32, name=f"b_far{t}", align_bytes=64) for t in range(PACK)]
        a_far = [keep.tile([P, S], F32, name=f"a_far{t}", align_bytes=64) for t in range(PACK)]
        low = [keep.tile([P, S], F32, name=f"low{t}", align_bytes=64) for t in range(PACK)]
        gap = [keep.tile([P, S], F32, name=f"gap{t}", align_bytes=64) for t in range(PACK)]

        def spans(t):
            return halves if t == PACK - 1 else [(0, S)]

        def leave_b(t):
            b0 = start_of(t, 0)
            nc.scalar.copy(scores[:, b0 : b0 + S], b_acc[t][:])

        def leave_a(t):
            a0 = start_of(t, 1)
            nc.scalar.copy(scores[:, a0 : a0 + S], a_acc[t][:])

        def fetch_b(t):
            b0 = start_of(t, 0)
            for lo, hi in spans(t):
                picked = scores[:, b0 : b0 + 2 * S].indirect(n2_t[:, lo // 16 : hi // 16])
                nc.scalar.activation(b_far[t][:, lo:hi], picked, COPY)

        def fetch_a(t):
            a0 = start_of(t, 1)
            picked = scores[:, a0 : a0 + 2 * S].indirect(n1_t[:])
            if t < 3:
                nc.vector.tensor_copy(a_far[t][:], picked)
            else:
                nc.scalar.activation(a_far[t][:], picked, COPY)

        def larger(t):
            a0 = start_of(t, 1)
            for lo, hi in spans(t):
                nc.vector.tensor_tensor(h_win[t][:, S + lo : S + hi], scores[:, a0 + lo : a0 + hi], b_far[t][:, lo:hi], ALU.max)

        def smaller(t):
            b0 = start_of(t, 0)
            nc.vector.tensor_tensor(low[t][:], a_far[t][:], scores[:, b0 : b0 + S], ALU.min)

        def subtract(t):
            for lo, hi in spans(t):
                nc.vector.tensor_tensor(gap[t][:, lo:hi], h_win[t][:, S + lo : S + hi], low[t][:, lo:hi], ALU.subtract)

        def scale(t):
            for lo, hi in spans(t):
                nc.vector.tensor_scalar(z_rows[:, t, lo:hi], gap[t][:, lo:hi], gain[:, t, 0:1], 0.0625, ALU.mult, ALU.mult)

        leave_a(0)
        for t in range(PACK + 1):
            if t < PACK:
                leave_b(t)
            if t + 1 < PACK:
                leave_a(t + 1)
            if t < PACK:
                fetch_a(t)
                fetch_b(t)
                smaller(t)
            if t > 0:
                subtract(t - 1)
            if t < PACK:
                larger(t)
            if t > 0:
                scale(t - 1)

        freed = ["a_far3", "b_far3", "low3", "z_grouped"]
        w_grouped = {}
        w_codes = keep.tile([P, N], U32, name="w_codes", align_bytes=64)
        w_plane = keep.tile([P, N], U8, name="w_plane", align_bytes=64)
        w_view = w_raw.rearrange("p j (r t c i) -> p t r c j i", r=8, t=PACK, i=4)

        def group_w(t, copy):
            w_grouped[t] = keep.tile([P, P * PACK], BF16, name=f"w_grouped{t}", tag=freed[t], align_bytes=64)
            copy(w_grouped[t][:].rearrange("p (r c i j) -> p r c j i", r=8, i=4, j=PACK), w_view[:, t])

        def quantize_w(t):
            cols = slice(t * P, (t + 1) * P)
            nc.vector.quantize_mx(out=w_codes[:, cols].bitcast(FP8X4), scales=w_plane[:, cols], in_=w_grouped[t][:])

        for t in range(3):
            group_w(t, nc.scalar.copy)

        z_codes = keep.tile([P, S], U32, name="z_codes", align_bytes=64)
        z_plane = keep.tile([P, S], U8, name="z_plane", align_bytes=64)
        for lo, hi in halves:
            nc.vector.tensor_copy(
                z_grouped[:, lo * PACK : hi * PACK].rearrange("p (c i t) -> p c t i", i=4, t=PACK),
                z_rows[:, :, lo:hi].rearrange("p t (c i) -> p c t i", i=4),
            )
        quantize_w(0)
        for lo, hi in halves:
            nc.vector.quantize_mx(
                out=z_codes[:, lo:hi].bitcast(FP8X4), scales=z_plane[:, lo:hi], in_=z_grouped[:, lo * PACK : hi * PACK]
            )

        out_view = out.rearrange("(r t i) j -> t r i j", r=8, t=PACK)
        for t in range(PACK):
            cols = slice(t * P, (t + 1) * P)
            if t >= 3:
                group_w(t, nc.vector.tensor_copy)
            if t > 0:
                quantize_w(t)
            for u, (lo, hi) in enumerate(halves if t == 0 else [(0, S)]):
                acc = psum.tile([P, hi - lo], F32, name=f"h_acc{t}{u}", tag=f"bank{u}{t}")
                nc.tensor.matmul_mx(
                    out=acc[:],
                    lhsT=w_codes[:, cols].bitcast(FP8X4),
                    lhsT_scale=w_plane[:, cols],
                    rhs=z_codes[:, lo:hi].bitcast(FP8X4),
                    rhs_scale=z_plane[:, lo:hi],
                    start=True,
                    stop=True,
                )
                nc.vector.tensor_copy(h_win[t][:, lo:hi], acc[:])
        pieces = [(t, 0, S) for t in range(PACK - 1)] + [(PACK - 1, 0, half), (PACK - 1, half, S)]
        for t, lo, hi in pieces:
            h3 = keep.tile([P, hi - lo], F32, name=f"h3_{t}_{lo}")
            h4 = keep.tile([P, hi - lo], F32, name=f"h4_{t}_{lo}")
            top = keep.tile([P, hi - lo], F32, name=f"top{t}_{lo}")
            res = keep.tile([P, hi - lo], F32, name=f"res{t}_{lo}")
            nc.scalar.activation(h3[:], h_win[t][:].indirect(n3_t[:, lo // 16 : hi // 16]), COPY)
            nc.scalar.activation(h4[:], h_win[t][:].indirect(n4_t[:, lo // 16 : hi // 16]), COPY)
            nc.vector.tensor_tensor(top[:], h3[:], h4[:], ALU.max)
            nc.vector.scalar_tensor_tensor(res[:], h_win[t][:, lo:hi], -0.75, top[:], ALU.mult, ALU.add)
            nc.sync.dma_start(out_view[t][:, :, lo:hi], res[:])
